import numpy as np
import ml_dtypes

BF16 = ml_dtypes.bfloat16


def bf(x):
    return np.asarray(x, np.float32).astype(BF16)


def f32(x):
    return np.asarray(x, np.float32)


def f64(x):
    return np.asarray(x).astype(np.float64)


def striped(idx):
    return np.concatenate([l.reshape(-1, 16).T for l in idx])


def rows(idx, k):
    return np.tile(np.repeat(idx, 16, axis=0), (k // (16 * 8), 1))


def look(tab, idx):
    return np.take_along_axis(f64(tab), rows(idx, len(tab)), axis=1)


K, S, V, N = 128, 2048, 2048, 2048


def setup_inputs():
    return {"tab": f32(np.random.standard_normal((2, K, S))), "y": f32(np.random.standard_normal((K, V))), "offs": striped(np.stack([np.random.permutation(S)[:N] for _ in range(8)]))}


def reference(tab, y, offs):
    idx = np.stack([g.T.reshape(-1) for g in np.split(offs, 8)])
    x = (look(tab[0], idx) - f64(y)) * (np.maximum(look(tab[1], idx), 0.0))
    return x

@@ -1,0 +1,46 @@
+import concourse.mybir as mybir
+
+F32, U16 = mybir.dt.float32, mybir.dt.uint16
+RELU = mybir.ActivationFunctionType.Relu
+SUBTRACT, MULT = mybir.AluOpType.subtract, mybir.AluOpType.mult
+
+P = 128
+PLACES = 2048
+N = 2048
+PIECE = 512
+PIECES = N // PIECE
+LIST_COLUMNS = PIECE // 16
+
+
+def tile_lookup_vg_subrelu_out_kernel(tc, tab, y, offs, out):
+    nc = tc.nc
+    with (
+        tc.tile_pool(name="held", bufs=1) as held,
+        tc.tile_pool(name="pieces", bufs=PIECES) as pieces,
+    ):
+        offsets = held.tile([P, N // 16], U16, name="offsets")
+        values = held.tile([P, PLACES], F32, name="values")
+        gates = held.tile([P, PLACES], F32, name="gates")
+        stream = held.tile([P, N], F32, name="stream")
+
+        nc.sync.dma_start(offsets[:], offs)
+        nc.sync.dma_start(values[:], tab[0])
+        nc.sync.dma_start(stream[:], y)
+        nc.sync.dma_start(gates[:], tab[1])
+
+        differences = []
+        for i in range(PIECES):
+            columns = slice(i * PIECE, (i + 1) * PIECE)
+            listed = offsets[:, i * LIST_COLUMNS : (i + 1) * LIST_COLUMNS]
+            difference = pieces.tile([P, PIECE], F32, name="difference")
+            nc.vector.tensor_tensor(difference[:], values[:].indirect(listed), stream[:, columns], SUBTRACT)
+            differences.append(difference)
+
+        for i in range(PIECES):
+            columns = slice(i * PIECE, (i + 1) * PIECE)
+            listed = offsets[:, i * LIST_COLUMNS : (i + 1) * LIST_COLUMNS]
+            gate = pieces.tile([P, PIECE], F32, name="gate")
+            nc.scalar.activation(gate[:], gates[:].indirect(listed), RELU)
+            x = pieces.tile([P, PIECE], F32, name="x")
+            nc.vector.tensor_tensor(x[:], differences[i][:], gate[:], MULT)
+            nc.sync.dma_start(out[:, columns], x[:])

@@ -9,6 +9,7 @@ PLACES = 2048
 N = 2048
 PIECE = 512
 PIECES = N // PIECE
+HALF = N // 2
 LIST_COLUMNS = PIECE // 16
 
 
@@ -21,19 +22,26 @@ def tile_lookup_vg_subrelu_out_kernel(tc, tab, y, offs, out):
         offsets = held.tile([P, N // 16], U16, name="offsets")
         values = held.tile([P, PLACES], F32, name="values")
         gates = held.tile([P, PLACES], F32, name="gates")
-        stream = held.tile([P, N], F32, name="stream")
+        stream = [held.tile([P, HALF], F32, name=f"stream{h}") for h in range(2)]
 
         nc.sync.dma_start(offsets[:], offs)
         nc.sync.dma_start(values[:], tab[0])
-        nc.sync.dma_start(stream[:], y)
+        nc.sync.dma_start(stream[0][:], y[:, :HALF])
         nc.sync.dma_start(gates[:], tab[1])
+        nc.sync.dma_start(stream[1][:], y[:, HALF:])
+
+        warm = held.tile([P, 1], F32, name="warm")
+        nc.vector.memset(warm[:], 0.0)
+        nc.scalar.activation(warm[:], warm[:], RELU)
 
         differences = []
         for i in range(PIECES):
-            columns = slice(i * PIECE, (i + 1) * PIECE)
+            h, start = divmod(i * PIECE, HALF)
             listed = offsets[:, i * LIST_COLUMNS : (i + 1) * LIST_COLUMNS]
             difference = pieces.tile([P, PIECE], F32, name="difference")
-            nc.vector.tensor_tensor(difference[:], values[:].indirect(listed), stream[:, columns], SUBTRACT)
+            nc.vector.tensor_tensor(
+                difference[:], values[:].indirect(listed), stream[h][:, start : start + PIECE], SUBTRACT
+            )
             differences.append(difference)
 
         for i in range(PIECES):

@@ -9,7 +9,6 @@ PLACES = 2048
 N = 2048
 PIECE = 512
 PIECES = N // PIECE
-HALF = N // 2
 LIST_COLUMNS = PIECE // 16
 
 
@@ -22,13 +21,15 @@ def tile_lookup_vg_subrelu_out_kernel(tc, tab, y, offs, out):
         offsets = held.tile([P, N // 16], U16, name="offsets")
         values = held.tile([P, PLACES], F32, name="values")
         gates = held.tile([P, PLACES], F32, name="gates")
-        stream = [held.tile([P, HALF], F32, name=f"stream{h}") for h in range(2)]
+        stream = [held.tile([P, PIECE], F32, name=f"stream{i}") for i in range(PIECES)]
 
         nc.sync.dma_start(offsets[:], offs)
         nc.sync.dma_start(values[:], tab[0])
-        nc.sync.dma_start(stream[0][:], y[:, :HALF])
+        for i in range(PIECES // 2):
+            nc.sync.dma_start(stream[i][:], y[:, i * PIECE : (i + 1) * PIECE])
         nc.sync.dma_start(gates[:], tab[1])
-        nc.sync.dma_start(stream[1][:], y[:, HALF:])
+        for i in range(PIECES // 2, PIECES):
+            nc.sync.dma_start(stream[i][:], y[:, i * PIECE : (i + 1) * PIECE])
 
         warm = held.tile([P, 1], F32, name="warm")
         nc.vector.memset(warm[:], 0.0)
@@ -36,12 +37,9 @@ def tile_lookup_vg_subrelu_out_kernel(tc, tab, y, offs, out):
 
         differences = []
         for i in range(PIECES):
-            h, start = divmod(i * PIECE, HALF)
             listed = offsets[:, i * LIST_COLUMNS : (i + 1) * LIST_COLUMNS]
             difference = pieces.tile([P, PIECE], F32, name="difference")
-            nc.vector.tensor_tensor(
-                difference[:], values[:].indirect(listed), stream[h][:, start : start + PIECE], SUBTRACT
-            )
+            nc.vector.tensor_tensor(difference[:], values[:].indirect(listed), stream[i][:], SUBTRACT)
             differences.append(difference)
 
         for i in range(PIECES):

@@ -43,10 +43,12 @@ def tile_lookup_vg_subrelu_out_kernel(tc, tab, y, offs, out):
             differences.append(difference)
 
         for i in range(PIECES):
-            columns = slice(i * PIECE, (i + 1) * PIECE)
             listed = offsets[:, i * LIST_COLUMNS : (i + 1) * LIST_COLUMNS]
             gate = pieces.tile([P, PIECE], F32, name="gate")
             nc.scalar.activation(gate[:], gates[:].indirect(listed), RELU)
             x = pieces.tile([P, PIECE], F32, name="x")
-            nc.vector.tensor_tensor(x[:], differences[i][:], gate[:], MULT)
-            nc.sync.dma_start(out[:, columns], x[:])
+            width = PIECE if i < PIECES - 1 else PIECE // 2
+            for start in range(0, PIECE, width):
+                part = slice(start, start + width)
+                nc.vector.tensor_tensor(x[:, part], differences[i][:, part], gate[:, part], MULT)
+                nc.sync.dma_start(out[:, i * PIECE + start : i * PIECE + start + width], x[:, part])

import concourse.mybir as mybir

F32, U16 = mybir.dt.float32, mybir.dt.uint16
RELU = mybir.ActivationFunctionType.Relu
SUBTRACT, MULT = mybir.AluOpType.subtract, mybir.AluOpType.mult

P = 128
PLACES = 2048
N = 2048
PIECE = 512
PIECES = N // PIECE
LIST_COLUMNS = PIECE // 16


def tile_lookup_vg_subrelu_out_kernel(tc, tab, y, offs, out):
    nc = tc.nc
    with (
        tc.tile_pool(name="held", bufs=1) as held,
        tc.tile_pool(name="pieces", bufs=PIECES) as pieces,
    ):
        offsets = held.tile([P, N // 16], U16, name="offsets")
        values = held.tile([P, PLACES], F32, name="values")
        gates = held.tile([P, PLACES], F32, name="gates")
        stream = [held.tile([P, PIECE], F32, name=f"stream{i}") for i in range(PIECES)]

        nc.sync.dma_start(offsets[:], offs)
        nc.sync.dma_start(values[:], tab[0])
        for i in range(PIECES // 2):
            nc.sync.dma_start(stream[i][:], y[:, i * PIECE : (i + 1) * PIECE])
        nc.sync.dma_start(gates[:], tab[1])
        for i in range(PIECES // 2, PIECES):
            nc.sync.dma_start(stream[i][:], y[:, i * PIECE : (i + 1) * PIECE])

        warm = held.tile([P, 1], F32, name="warm")
        nc.vector.memset(warm[:], 0.0)
        nc.scalar.activation(warm[:], warm[:], RELU)

        differences = []
        for i in range(PIECES):
            listed = offsets[:, i * LIST_COLUMNS : (i + 1) * LIST_COLUMNS]
            difference = pieces.tile([P, PIECE], F32, name="difference")
            nc.vector.tensor_tensor(difference[:], values[:].indirect(listed), stream[i][:], SUBTRACT)
            differences.append(difference)

        for i in range(PIECES):
            listed = offsets[:, i * LIST_COLUMNS : (i + 1) * LIST_COLUMNS]
            gate = pieces.tile([P, PIECE], F32, name="gate")
            nc.scalar.activation(gate[:], gates[:].indirect(listed), RELU)
            x = pieces.tile([P, PIECE], F32, name="x")
            width = PIECE if i < PIECES - 1 else PIECE // 2
            for start in range(0, PIECE, width):
                part = slice(start, start + width)
                nc.vector.tensor_tensor(x[:, part], differences[i][:, part], gate[:, part], MULT)
                nc.sync.dma_start(out[:, i * PIECE + start : i * PIECE + start + width], x[:, part])
